import numpy as np
import ml_dtypes

BF16 = ml_dtypes.bfloat16


def bf(x):
    return np.asarray(x, np.float32).astype(BF16)


def f32(x):
    return np.asarray(x, np.float32)


def f64(x):
    return np.asarray(x).astype(np.float64)


def striped(idx):
    return np.concatenate([l.reshape(-1, 16).T for l in idx])


def rows(idx, k):
    return np.tile(np.repeat(idx, 16, axis=0), (k // (16 * 8), 1))


def look(tab, idx):
    return np.take_along_axis(f64(tab), rows(idx, len(tab)), axis=1)


K, S, D, V, N, M = 128, 2048, 3, 512, 1536, 128


def setup_inputs():
    return {"tab": f32(np.random.standard_normal((K, S))), "ctr": f32(np.random.standard_normal((K, V))), "w": bf(np.random.standard_normal((K, M)) / np.sqrt(K)), "offs": striped(np.stack([np.random.permutation(S)[:N] for _ in range(8)]))}


def reference(tab, ctr, w, offs):
    idx = np.stack([g.T.reshape(-1) for g in np.split(offs, 8)])
    x = sum(np.maximum(look(tab, idx[:, d * V:(d + 1) * V]) - f64(ctr), 0.0) for d in range(D))
    y = f64(w).T @ x
    return y

@@ -1,0 +1,41 @@
+import concourse.mybir as mybir
+
+F32, BF16, U16 = mybir.dt.float32, mybir.dt.bfloat16, mybir.dt.uint16
+ADD, MAX, SUBTRACT = mybir.AluOpType.add, mybir.AluOpType.max, mybir.AluOpType.subtract
+
+ROWS, TABLE, NEIGHBOURS, CENTRES, OUTS = 128, 2048, 3, 512, 128
+LIST_COLUMNS = CENTRES // 16
+
+FLOPS = 2 * ROWS * OUTS * CENTRES
+
+
+def tile_lookup_edge_sub_none_kernel(tc, tab, ctr, w, offs, out):
+    nc = tc.nc
+    with tc.tile_pool(name="held", bufs=1) as held, tc.psum_pool(name="psum", bufs=1) as psum:
+        offsets = held.tile([ROWS, NEIGHBOURS * LIST_COLUMNS], U16, name="offsets")
+        table = held.tile([ROWS, TABLE], F32, name="table")
+        centre = held.tile([ROWS, CENTRES], F32, name="centre")
+        weights = held.tile([ROWS, OUTS], BF16, name="weights")
+        nc.sync.dma_start(offsets[:], offs)
+        nc.sync.dma_start(table[:], tab)
+        nc.scalar.dma_start(centre[:], ctr)
+        nc.scalar.dma_start(weights[:], w)
+
+        x = None
+        for d in range(NEIGHBOURS):
+            picked = table[:].indirect(offsets[:, d * LIST_COLUMNS : (d + 1) * LIST_COLUMNS])
+            difference = held.tile([ROWS, CENTRES], F32, name=f"difference{d}")
+            nc.vector.tensor_tensor(difference[:], picked, centre[:], SUBTRACT)
+            last = d == NEIGHBOURS - 1
+            longer_sum = held.tile([ROWS, CENTRES], BF16 if last else F32, name=f"sum{d}")
+            if x is None:
+                nc.vector.tensor_scalar_max(longer_sum[:], difference[:], 0.0)
+            else:
+                nc.vector.scalar_tensor_tensor(longer_sum[:], difference[:], 0.0, x[:], MAX, ADD)
+            x = longer_sum
+
+        product = psum.tile([OUTS, CENTRES], F32, name="product")
+        nc.tensor.matmul(product[:], weights[:], x[:], start=True, stop=True)
+        result = held.tile([OUTS, CENTRES], F32, name="result")
+        nc.scalar.copy(result[:], product[:])
+        nc.sync.dma_start(out, result[:])

@@ -1,7 +1,8 @@
 import concourse.mybir as mybir
 
 F32, BF16, U16 = mybir.dt.float32, mybir.dt.bfloat16, mybir.dt.uint16
-ADD, MAX, SUBTRACT = mybir.AluOpType.add, mybir.AluOpType.max, mybir.AluOpType.subtract
+SUBTRACT = mybir.AluOpType.subtract
+RELU = mybir.ActivationFunctionType.Relu
 
 ROWS, TABLE, NEIGHBOURS, CENTRES, OUTS = 128, 2048, 3, 512, 128
 LIST_COLUMNS = CENTRES // 16
@@ -21,21 +22,15 @@ def tile_lookup_edge_sub_none_kernel(tc, tab, ctr, w, offs, out):
         nc.scalar.dma_start(centre[:], ctr)
         nc.scalar.dma_start(weights[:], w)
 
-        x = None
+        product = psum.tile([OUTS, CENTRES], F32, name="product")
         for d in range(NEIGHBOURS):
             picked = table[:].indirect(offsets[:, d * LIST_COLUMNS : (d + 1) * LIST_COLUMNS])
             difference = held.tile([ROWS, CENTRES], F32, name=f"difference{d}")
             nc.vector.tensor_tensor(difference[:], picked, centre[:], SUBTRACT)
-            last = d == NEIGHBOURS - 1
-            longer_sum = held.tile([ROWS, CENTRES], BF16 if last else F32, name=f"sum{d}")
-            if x is None:
-                nc.vector.tensor_scalar_max(longer_sum[:], difference[:], 0.0)
-            else:
-                nc.vector.scalar_tensor_tensor(longer_sum[:], difference[:], 0.0, x[:], MAX, ADD)
-            x = longer_sum
+            term = held.tile([ROWS, CENTRES], BF16, name=f"term{d}")
+            nc.scalar.activation(term[:], difference[:], RELU)
+            nc.tensor.matmul(product[:], weights[:], term[:], start=d == 0, stop=d == NEIGHBOURS - 1)
 
-        product = psum.tile([OUTS, CENTRES], F32, name="product")
-        nc.tensor.matmul(product[:], weights[:], x[:], start=True, stop=True)
         result = held.tile([OUTS, CENTRES], F32, name="result")
         nc.scalar.copy(result[:], product[:])
         nc.sync.dma_start(out, result[:])

@@ -5,6 +5,7 @@ SUBTRACT = mybir.AluOpType.subtract
 RELU = mybir.ActivationFunctionType.Relu
 
 ROWS, TABLE, NEIGHBOURS, CENTRES, OUTS = 128, 2048, 3, 512, 128
+HALF = CENTRES // 2
 LIST_COLUMNS = CENTRES // 16
 
 FLOPS = 2 * ROWS * OUTS * CENTRES
@@ -22,15 +23,23 @@ def tile_lookup_edge_sub_none_kernel(tc, tab, ctr, w, offs, out):
         nc.scalar.dma_start(centre[:], ctr)
         nc.scalar.dma_start(weights[:], w)
 
-        product = psum.tile([OUTS, CENTRES], F32, name="product")
+        halves = [slice(0, HALF), slice(HALF, CENTRES)]
+        products = [psum.tile([OUTS, HALF], F32, name=f"product{h}") for h in range(2)]
         for d in range(NEIGHBOURS):
+            first, last = d == 0, d == NEIGHBOURS - 1
             picked = table[:].indirect(offsets[:, d * LIST_COLUMNS : (d + 1) * LIST_COLUMNS])
             difference = held.tile([ROWS, CENTRES], F32, name=f"difference{d}")
             nc.vector.tensor_tensor(difference[:], picked, centre[:], SUBTRACT)
-            term = held.tile([ROWS, CENTRES], BF16, name=f"term{d}")
-            nc.scalar.activation(term[:], difference[:], RELU)
-            nc.tensor.matmul(product[:], weights[:], term[:], start=d == 0, stop=d == NEIGHBOURS - 1)
+            terms = [held.tile([ROWS, HALF], BF16, name=f"term{d}_{h}") for h in range(2)]
+            for term, product, half in zip(terms, products, halves):
+                if last:
+                    nc.vector.tensor_scalar_max(term[:], difference[:, half], 0.0)
+                else:
+                    nc.scalar.activation(term[:], difference[:, half], RELU)
+                nc.tensor.matmul(product[:], weights[:], term[:], start=first, stop=last)
 
-        result = held.tile([OUTS, CENTRES], F32, name="result")
-        nc.scalar.copy(result[:], product[:])
-        nc.sync.dma_start(out, result[:])
+        results = [held.tile([OUTS, HALF], F32, name=f"result{h}") for h in range(2)]
+        nc.scalar.copy(results[0][:], products[0][:])
+        nc.sync.dma_start(out[:, halves[0]], results[0][:])
+        nc.vector.tensor_copy(results[1][:], products[1][:])
+        nc.scalar.dma_start(out[:, halves[1]], results[1][:])

@@ -19,8 +19,9 @@ def tile_lookup_edge_sub_none_kernel(tc, tab, ctr, w, offs, out):
         centre = held.tile([ROWS, CENTRES], F32, name="centre")
         weights = held.tile([ROWS, OUTS], BF16, name="weights")
         nc.sync.dma_start(offsets[:], offs)
-        nc.sync.dma_start(table[:], tab)
-        nc.scalar.dma_start(centre[:], ctr)
+        nc.sync.dma_start(table[:, : TABLE // 2], tab[:, : TABLE // 2])
+        nc.scalar.dma_start(table[:, TABLE // 2 :], tab[:, TABLE // 2 :])
+        nc.sync.dma_start(centre[:], ctr)
         nc.scalar.dma_start(weights[:], w)
 
         halves = [slice(0, HALF), slice(HALF, CENTRES)]

@@ -6,6 +6,7 @@ RELU = mybir.ActivationFunctionType.Relu
 
 ROWS, TABLE, NEIGHBOURS, CENTRES, OUTS = 128, 2048, 3, 512, 128
 HALF = CENTRES // 2
+WARM_UPS = 20
 LIST_COLUMNS = CENTRES // 16
 
 FLOPS = 2 * ROWS * OUTS * CENTRES
@@ -23,6 +24,12 @@ def tile_lookup_edge_sub_none_kernel(tc, tab, ctr, w, offs, out):
         nc.scalar.dma_start(table[:, TABLE // 2 :], tab[:, TABLE // 2 :])
         nc.sync.dma_start(centre[:], ctr)
         nc.scalar.dma_start(weights[:], w)
+
+        zeros = held.tile([ROWS, CENTRES], BF16, name="zeros")
+        nc.gpsimd.memset(zeros[:], 0.0)
+        unread = psum.tile([OUTS, CENTRES], F32, name="unread")
+        for repeat in range(WARM_UPS):
+            nc.tensor.matmul(unread[:], zeros[:, :OUTS], zeros[:], start=True, stop=True)
 
         halves = [slice(0, HALF), slice(HALF, CENTRES)]
         products = [psum.tile([OUTS, HALF], F32, name=f"product{h}") for h in range(2)]

import concourse.mybir as mybir

F32, BF16, U16 = mybir.dt.float32, mybir.dt.bfloat16, mybir.dt.uint16
SUBTRACT = mybir.AluOpType.subtract
RELU = mybir.ActivationFunctionType.Relu

ROWS, TABLE, NEIGHBOURS, CENTRES, OUTS = 128, 2048, 3, 512, 128
HALF = CENTRES // 2
WARM_UPS = 20
LIST_COLUMNS = CENTRES // 16

FLOPS = 2 * ROWS * OUTS * CENTRES


def tile_lookup_edge_sub_none_kernel(tc, tab, ctr, w, offs, out):
    nc = tc.nc
    with tc.tile_pool(name="held", bufs=1) as held, tc.psum_pool(name="psum", bufs=1) as psum:
        offsets = held.tile([ROWS, NEIGHBOURS * LIST_COLUMNS], U16, name="offsets")
        table = held.tile([ROWS, TABLE], F32, name="table")
        centre = held.tile([ROWS, CENTRES], F32, name="centre")
        weights = held.tile([ROWS, OUTS], BF16, name="weights")
        nc.sync.dma_start(offsets[:], offs)
        nc.sync.dma_start(table[:, : TABLE // 2], tab[:, : TABLE // 2])
        nc.scalar.dma_start(table[:, TABLE // 2 :], tab[:, TABLE // 2 :])
        nc.sync.dma_start(centre[:], ctr)
        nc.scalar.dma_start(weights[:], w)

        zeros = held.tile([ROWS, CENTRES], BF16, name="zeros")
        nc.gpsimd.memset(zeros[:], 0.0)
        unread = psum.tile([OUTS, CENTRES], F32, name="unread")
        for repeat in range(WARM_UPS):
            nc.tensor.matmul(unread[:], zeros[:, :OUTS], zeros[:], start=True, stop=True)

        halves = [slice(0, HALF), slice(HALF, CENTRES)]
        products = [psum.tile([OUTS, HALF], F32, name=f"product{h}") for h in range(2)]
        for d in range(NEIGHBOURS):
            first, last = d == 0, d == NEIGHBOURS - 1
            picked = table[:].indirect(offsets[:, d * LIST_COLUMNS : (d + 1) * LIST_COLUMNS])
            difference = held.tile([ROWS, CENTRES], F32, name=f"difference{d}")
            nc.vector.tensor_tensor(difference[:], picked, centre[:], SUBTRACT)
            terms = [held.tile([ROWS, HALF], BF16, name=f"term{d}_{h}") for h in range(2)]
            for term, product, half in zip(terms, products, halves):
                if last:
                    nc.vector.tensor_scalar_max(term[:], difference[:, half], 0.0)
                else:
                    nc.scalar.activation(term[:], difference[:, half], RELU)
                nc.tensor.matmul(product[:], weights[:], term[:], start=first, stop=last)

        results = [held.tile([OUTS, HALF], F32, name=f"result{h}") for h in range(2)]
        nc.scalar.copy(results[0][:], products[0][:])
        nc.sync.dma_start(out[:, halves[0]], results[0][:])
        nc.vector.tensor_copy(results[1][:], products[1][:])
        nc.scalar.dma_start(out[:, halves[1]], results[1][:])
